import numpy as np
import ml_dtypes


def mxq(x, axis, fmt="e4m3"):
    dtype, down = {"e4m3": (ml_dtypes.float8_e4m3fn, 7), "e5m2": (ml_dtypes.float8_e5m2, 14)}[fmt]
    v = np.moveaxis(np.asarray(x, np.float32).astype(ml_dtypes.bfloat16).astype(np.float64), axis, -1)
    blocks = v.reshape(v.shape[:-1] + (-1, 32))
    amax = np.abs(blocks).max(-1, keepdims=True)
    byte = np.maximum(np.where(amax > 0, np.frexp(amax)[1] - 1 + 127, 0) - down, 1)
    scale = np.exp2(byte - 127.0)
    codes = (blocks / scale).astype(np.float32).astype(dtype).astype(np.float64)
    return np.moveaxis((codes * scale).reshape(v.shape), -1, axis)


WIDE = False


def mx_kscale(k):
    if not WIDE:
        return np.ones(k)
    levels = np.array([10, -10, 5, -5, 0])
    if k % 512:
        return np.exp2(np.random.permutation(np.resize(levels, k // 32))).repeat(32)
    a = np.empty((k // 512, 16))
    for p in range(k // 512):
        a[p, :8] = np.random.permutation(np.resize(levels, 8))
        for g in range(8):
            far = levels[np.abs(levels - a[p, g]) >= 10]
            a[p, g + 8] = far[np.random.randint(len(far))]
    return np.exp2(a.ravel()).repeat(32)


def f64(x):
    return np.asarray(x).astype(np.float64)


def striped(idx):
    return np.tile(idx.reshape(-1, 16).T, (8, 1)).astype(np.uint16)


def unstriped(offs):
    return offs[:16].T.reshape(-1).astype(np.int64)


E2M1 = np.array([0.0, 0.5, 1.0, 1.5, 2.0, 3.0, 4.0, 6.0, -0.0, -0.5, -1.0, -1.5, -2.0, -3.0, -4.0, -6.0])


def pack_weight(w, fmt):
    k, n = w.shape
    w = f64(np.asarray(w, np.float32).astype(ml_dtypes.bfloat16)).reshape(k // 32, 32, n)
    amax = np.abs(w).max(1)
    if fmt == "e4m3":
        byte = np.frexp(amax)[1] - 1 + 127 - 7
    else:
        mant, ex = np.frexp(amax / 6.0)
        byte = np.where(mant > 0.5, ex, ex - 1) + 127
    byte = np.clip(np.where(amax > 0, byte, 1), 1, 254)
    scaled = (w * np.exp2(127.0 - byte)[:, None, :]).reshape(k, n).astype(np.float32)
    by_word = np.ascontiguousarray(scaled.reshape(k // 512, 128, 4, n).transpose(0, 1, 3, 2))
    if fmt == "e4m3":
        words = by_word.astype(ml_dtypes.float8_e4m3fn).view(np.uint8)
    else:
        c = by_word.astype(ml_dtypes.float4_e2m1fn).view(np.uint8) & 0xF
        words = (c[..., 0::2] | (c[..., 1::2] << 4)).reshape(k // 512, 128, 2 * n)
    return np.ascontiguousarray(words), np.ascontiguousarray(byte.astype(np.uint8).reshape(k // 512, 16, n))


def unpack_weight(words, scales, fmt):
    g, _, n = scales.shape
    words = np.ascontiguousarray(words).reshape(g, 128, n, -1)
    if fmt == "e4m3":
        vals = words.view(ml_dtypes.float8_e4m3fn).astype(np.float64)
    else:
        nib = np.empty((g, 128, n, 4), np.uint8)
        nib[..., 0::2] = words & 0xF
        nib[..., 1::2] = words >> 4
        vals = E2M1[nib]
    vals = vals * np.repeat(np.exp2(scales.astype(np.float64) - 127.0), 8, axis=1)[..., None]
    return vals.transpose(0, 1, 3, 2).reshape(g * 512, n)


K, T, E, C, N, TOP = 256, 512, 16, 128, 512, 4


def by_expert(wq, xq):
    return np.concatenate([wq[e].T @ xq[:, e * C:(e + 1) * C] for e in range(E)], axis=1)


def setup_inputs():
    n = np.random.standard_normal
    v = mx_kscale(N)
    deal = np.repeat(np.arange(E), C).reshape(TOP, T)[:, np.random.permutation(T)]
    deal = np.take_along_axis(deal, np.argsort(np.random.rand(TOP, T), axis=0), axis=0)
    for _ in range(8):
        s_, t_ = np.random.permutation(T).reshape(2, -1); r = np.random.randint(TOP, size=T // 2); x, y = deal[r, s_].copy(), deal[r, t_].copy()
        ok = ~((deal[:, s_] == y).any(0) | (deal[:, t_] == x).any(0)); deal[r[ok], s_[ok]] = y[ok]; deal[r[ok], t_[ok]] = x[ok]
    order = np.argsort(deal.reshape(-1) + 0.5 * np.random.rand(TOP * T))
    slot_token = order % T; pos = np.empty(TOP * T, np.int64); pos[order] = np.arange(TOP * T); pos = pos.reshape(TOP, T)
    g = np.random.uniform(0.5, 1.5, (TOP, T)); g = g / g.sum(0)
    w_slot = np.empty(E * C)
    for r in range(TOP): w_slot[pos[r]] = g[r]
    dq = pack_weight(n((N, T)) * v[:, None], "e4m3")
    dk = pack_weight(n((N, T)) * v[:, None], "e4m3")
    dv = pack_weight(n((N, T)) * v[:, None], "e4m3")
    wq = [pack_weight(m, "e2m1") for m in n((E, N, K)) / np.sqrt(N) / v[None, :, None]]
    wv = [pack_weight(m, "e2m1") for m in n((E, N, K)) / np.sqrt(N) / v[None, :, None]]
    return {
        "dq_words": dq[0],
        "dq_scales": dq[1],
        "dk_words": dk[0],
        "dk_scales": dk[1],
        "dv_words": dv[0],
        "dv_scales": dv[1],
        "wq_words": np.stack([m[0] for m in wq]),
        "wq_scales": np.stack([m[1] for m in wq]),
        "wk": (n((E, N, K)) / np.sqrt(N) / v[None, :, None]).astype(np.float32),
        "wv_words": np.stack([m[0] for m in wv]),
        "wv_scales": np.stack([m[1] for m in wv]),
        "gate": (np.tile(w_slot, (128, 1))).astype(np.float32),
        "offs": striped(slot_token),
        "pos1": striped(pos[0]),
        "pos2": striped(pos[1]),
        "pos3": striped(pos[2]),
        "pos4": striped(pos[3]),
    }


def reference(dq_words, dq_scales, dk_words, dk_scales, dv_words, dv_scales, wq_words, wq_scales, wk, wv_words, wv_scales, gate, offs, pos1, pos2, pos3, pos4):
    wq = np.stack([unpack_weight(wq_words[e], wq_scales[e], "e2m1") for e in range(E)])
    wkq = mxq(f64(wk), 1, "e4m3")
    wv = np.stack([unpack_weight(wv_words[e], wv_scales[e], "e2m1") for e in range(E)])
    idx = unstriped(offs)
    gq, gk, gv = [unpack_weight(w, s, "e4m3")[:, idx] for w, s in ((dq_words, dq_scales), (dk_words, dk_scales), (dv_words, dv_scales))]
    dx = f64(gate[:1]) * (by_expert(wq, gq) + by_expert(wkq, gk) + by_expert(wv, gv))
    out = dx[:, unstriped(pos1)] + dx[:, unstriped(pos2)] + dx[:, unstriped(pos3)] + dx[:, unstriped(pos4)]
    return out

@@ -1,0 +1,320 @@
+from contextlib import ExitStack
+
+import concourse.mybir as mybir
+from concourse.masks import make_identity
+
+K, T, E, C, N, TOP = 256, 512, 16, 128, 512, 4
+SLOTS = E * C
+FLOPS = 2 * 3 * SLOTS * N * K
+
+F32 = mybir.dt.float32
+BF16 = mybir.dt.bfloat16
+I32 = mybir.dt.int32
+U32 = mybir.dt.uint32
+U16 = mybir.dt.uint16
+U8 = mybir.dt.uint8
+FP8X4 = mybir.dt.float8_e4m3fn_x4
+FP4X4 = mybir.dt.float4_e2m1fn_x4
+COPY = mybir.ActivationFunctionType.Copy
+ADD = mybir.AluOpType.add
+
+P = 128
+WINDOW = 704
+LINE = 64
+CHUNKS = [(0, 4), (4, 4), (8, 4), (12, 2), (14, 2)]
+LATE = 12
+SCALE_SPAN = 8
+
+
+def lay_out(hosts):
+    place = {}
+    top = 0
+    for name, size, tenants in hosts:
+        lead = tenants[0][1] - LINE if tenants else 0
+        place[name] = top + lead
+        at = top
+        for tenant, tenant_size in tenants:
+            assert at < top + lead + size
+            place[tenant] = at
+            at = at + tenant_size
+        top = max(at, top + lead + size)
+    return place
+
+
+def tile_moe_qkb_kernel(
+    tc, dq_words, dq_scales, dk_words, dk_scales, dv_words, dv_scales, wq_words, wq_scales, wk, wv_words, wv_scales,
+    gate, offs, pos1, pos2, pos3, pos4, out,
+):
+    nc = tc.nc
+
+    def wsz(c):
+        return CHUNKS[c][1] * C * 4
+
+    def ssz(c):
+        return CHUNKS[c][1] * C
+
+    tenants = {
+        "bf1": [("gw1v", wsz(1)), ("gs1q", ssz(1)), ("gs1k", ssz(1)), ("gs1v", ssz(1))],
+        "bf3": [("gw2q", wsz(2)), ("gw2k", wsz(2)), ("gw2v", wsz(2))],
+        "bf4": [("gs2q", ssz(2)), ("gs2k", ssz(2))],
+        "bf5": [("gw3q", wsz(3)), ("gs2v", ssz(2)), ("gw3k", wsz(3)), ("gs3q", ssz(3)), ("gs3k", ssz(3)), ("gs3v", ssz(3)), ("gw3v", wsz(3))],
+        "raw13": [("gw4q", wsz(4)), ("gw4k", wsz(4)), ("gw4v", wsz(4))],
+        "raw15": [("gs4q", ssz(4)), ("gs4k", ssz(4)), ("gs4v", ssz(4)), ("y2", 4096)],
+        "raw7": [("y0", 4096)],
+        "raw11": [("y1", 4096)],
+        "swinv": [("late_codes", (E - LATE) * C * 4)],
+    }
+    hosts = [(f"raw{e}", 4096, tenants.get(f"raw{e}", [])) for e in range(E)]
+    hosts = hosts + [(f"bf{i}", 4096, tenants.get(f"bf{i}", [])) for i in range(E // 2)]
+    hosts = hosts + [("swinv", WINDOW, tenants["swinv"])]
+    place = lay_out(hosts)
+
+    with ExitStack() as ctx:
+        lists = ctx.enter_context(tc.tile_pool(name="lists", bufs=1))
+        keep = ctx.enter_context(tc.tile_pool(name="keep", bufs=1))
+        shared = ctx.enter_context(tc.tile_pool(name="shared", bufs=1))
+        psum = ctx.enter_context(tc.psum_pool(name="psum", bufs=1))
+
+        def new(name, shape, dtype):
+            if name in place:
+                return shared.tile(shape, dtype, name=name, offset=place[name], align_bytes=LINE)
+            return keep.tile(shape, dtype, name=name, align_bytes=LINE)
+
+        offs_sb = lists.tile([P, SLOTS // 16], U16, name="offs_sb")
+        pos_sb = [lists.tile([P, T // 16], U16, name=f"pos_sb{r}") for r in range(TOP)]
+
+        wwin = {x: new(f"wwin{x}", [P, WINDOW], I32) for x in "qkv"}
+        swin = {x: new(f"swin{x}", [P, WINDOW], U8) for x in "qkv"}
+        wplane = {(x, s): new(f"wplane{x}{s}", [P, SCALE_SPAN * K], U8) for x in "qv" for s in range(E // SCALE_SPAN)}
+        gate_rows = new("gate_rows", [P, C], F32)
+        ident = new("ident", [P, P], F32)
+
+        for x in "qkv":
+            nc.vector.memset(swin[x][:].bitcast(I32), 0)
+        nc.gpsimd.memset(gate_rows[:], 0.0)
+        for x in "qkv":
+            nc.vector.memset(wwin[x][:, T:], 0)
+        for x in "qv":
+            nc.vector.memset(wplane[x, 0][:].bitcast(I32), 0)
+        for x in "qv":
+            nc.gpsimd.memset(wplane[x, 1][:].bitcast(I32), 0)
+        make_identity(nc, ident[:])
+
+        words_in = {"q": dq_words, "k": dk_words, "v": dv_words}
+        scales_in = {"q": dq_scales, "k": dk_scales, "v": dv_scales}
+        w4_in = {"q": wq_words, "v": wv_words}
+        w4s_in = {"q": wq_scales, "v": wv_scales}
+        raw = {}
+        w4 = {}
+
+        def load_words(x):
+            nc.sync.dma_start(wwin[x][:, :T], words_in[x][0].rearrange("p t d -> p (t d)").bitcast(I32))
+
+        def load_scales(x):
+            src = scales_in[x][0].bitcast(I32).rearrange("(q r) t -> r q t", r=4)
+            for r in range(4):
+                nc.sync.dma_start(swin[x][:].bitcast(I32)[r:P:32, : T // 4], src[r])
+
+        def load_wk(e):
+            raw[e] = new(f"raw{e}", [P, 4, K], F32)
+            nc.sync.dma_start(raw[e][:], wk[e].rearrange("(p j) c -> p j c", j=4))
+
+        def load_w4(g):
+            for x in "qv":
+                w4[x, g] = new(f"w4{x}{g}", [P, 4 * 2 * K], U8)
+                src = w4_in[x][4 * g : 4 * g + 4, 0].bitcast(I32).rearrange("e p b -> p e b")
+                nc.sync.dma_start(w4[x, g][:].bitcast(I32).rearrange("p (e b) -> p e b", e=4), src)
+
+        def load_w4_scales(x, s):
+            src = w4s_in[x][SCALE_SPAN * s : SCALE_SPAN * (s + 1), 0].bitcast(I32).rearrange("e (q r) c -> r q e c", r=4)
+            dst = wplane[x, s][:].bitcast(I32).rearrange("p (e c) -> p e c", e=SCALE_SPAN)
+            for r in range(4):
+                nc.sync.dma_start(dst[r:P:32], src[r])
+
+        nc.sync.dma_start(offs_sb[:], offs)
+        load_words("q")
+        load_words("k")
+        nc.sync.dma_start(gate_rows[:E, :], gate[0:1, :].rearrange("o (e u) -> (o e) u", e=E))
+        load_words("v")
+        load_wk(0)
+        load_scales("q")
+        load_wk(1)
+        load_scales("k")
+        load_wk(2)
+        load_scales("v")
+        load_wk(3)
+        load_w4_scales("q", 0)
+        load_w4(0)
+        load_w4_scales("v", 0)
+        for e in range(4, 8):
+            load_wk(e)
+        load_w4(1)
+        for e in range(8, 12):
+            load_wk(e)
+        load_w4_scales("q", 1)
+        load_w4(2)
+        load_w4_scales("v", 1)
+        for e in range(12, 16):
+            load_wk(e)
+        load_w4(3)
+        for r, pos in enumerate((pos1, pos2, pos3, pos4)):
+            nc.sync.dma_start(pos_sb[r][:], pos)
+
+        gate_ps = psum.tile([P, P], F32, name="gate_ps", tag="tr", bufs=3)
+        nc.tensor.transpose(gate_ps[:], gate_rows[:], ident[:])
+        gate_col = new("gate_col", [P, E], F32)
+        nc.scalar.copy(gate_col[:], gate_ps[:, :E])
+
+        bf = {}
+        codes = {}
+        kscale = {}
+        gw = {}
+        gs = {}
+        y = {}
+        dx = [new(f"dx{h}", [P, SLOTS], F32) for h in range(2)]
+        late = {}
+
+        def cast(e):
+            i, j = divmod(e, 2)
+            if j == 0:
+                bf[i] = new(f"bf{i}", [P, 2, K, 4], BF16)
+            nc.scalar.copy(
+                bf[i][:, j].rearrange("p (c i) t -> p c t i", i=4),
+                raw[e][:].rearrange("p t (c i) -> p c t i", i=4),
+            )
+
+        def quant(i):
+            ct = new(f"codes{i}", [P, 2 * K], U32)
+            st = new(f"kscale{i}", [P, 2 * K], U8)
+            flat = bf[i][:].rearrange("p j c t -> p (j c t)")
+            if 2 * i < LATE:
+                nc.vector.quantize_mx(out=ct[:].bitcast(FP8X4), scales=st[:], in_=flat)
+            for j in range(2):
+                for h in range(2):
+                    if 2 * i < LATE or h == 0:
+                        cols = slice((2 * j + h) * C, (2 * j + h + 1) * C)
+                        codes[2 * i + j, h] = ct[:, cols]
+                        kscale[2 * i + j, h] = st[:, cols]
+                if 2 * i >= LATE:
+                    nc.vector.quantize_mx(out=codes[2 * i + j, 0].bitcast(FP8X4), scales=kscale[2 * i + j, 0],
+                                          in_=flat[:, 2 * j * 4 * C : (2 * j + 1) * 4 * C])
+
+        def quant_late():
+            late["codes"] = new("late_codes", [P, (E - LATE) * C], U32)
+            late["scales"] = new("late_scales", [P, (E - LATE) * C], U8)
+            for e in range(LATE, E):
+                i, j = divmod(e, 2)
+                cols = slice((e - LATE) * C, (e - LATE + 1) * C)
+                codes[e, 1] = late["codes"][:, cols]
+                kscale[e, 1] = late["scales"][:, cols]
+                flat = bf[i][:].rearrange("p j c t -> p (j c t)")
+                nc.vector.quantize_mx(out=codes[e, 1].bitcast(FP8X4), scales=kscale[e, 1],
+                                      in_=flat[:, (2 * j + 1) * 4 * C : (2 * j + 2) * 4 * C])
+
+        def chunk_offsets(c):
+            e0, ne = CHUNKS[c]
+            return offs_sb[:, e0 * C // 16 : (e0 + ne) * C // 16]
+
+        def gather_w(c, xs):
+            for x in xs:
+                gw[c, x] = new(f"gw{c}{x}", [P, CHUNKS[c][1] * C], U32)
+                nc.vector.tensor_copy(gw[c, x][:], wwin[x][:].bitcast(U32).indirect(chunk_offsets(c)))
+
+        def gather_s(c, xs):
+            for x in xs:
+                gs[c, x] = new(f"gs{c}{x}", [P, CHUNKS[c][1] * C], U8)
+                nc.vector.tensor_copy(gs[c, x][:], swin[x][:].indirect(chunk_offsets(c)))
+
+        def mx_pass(c, e, h, x, acc):
+            slots = slice((e - CHUNKS[c][0]) * C, (e - CHUNKS[c][0] + 1) * C)
+            if x == "k":
+                rhs, rhs_scale = codes[e, h].bitcast(FP8X4), kscale[e, h]
+            else:
+                b0 = (e % 4) * 2 * K + h * 2 * C
+                rhs = w4[x, e // 4][:, b0 : b0 + 2 * C].bitcast(FP4X4)
+                s0 = (e % SCALE_SPAN) * K + h * C
+                rhs_scale = wplane[x, e // SCALE_SPAN][:, s0 : s0 + C]
+            nc.tensor.matmul_mx(out=acc, lhsT=gw[c, x][:, slots].bitcast(FP8X4), lhsT_scale=gs[c, x][:, slots],
+                                rhs=rhs, rhs_scale=rhs_scale, start=(x == "q"), stop=(x == "v"))
+
+        def products(c, halves):
+            e0, ne = CHUNKS[c]
+            width = len(halves) * C
+            name = f"y{c}" if len(halves) == 2 else f"y{c}h{halves[0]}"
+            yt = new(name, [P, ne, width], F32)
+            if len(halves) == 2:
+                for e in range(e0, e0 + ne):
+                    acc = psum.tile([P, width], F32, name="acc", tag="acc", bufs=4)
+                    for h in halves:
+                        for x in "qkv":
+                            mx_pass(c, e, h, x, acc[:, h * C : (h + 1) * C])
+                    nc.scalar.activation(yt[:, e - e0], acc[:], COPY, scale=gate_col[:, e : e + 1])
+            else:
+                accs = [psum.tile([P, width], F32, name="acc", tag="acc", bufs=4) for e in range(ne)]
+                for x in "qkv":
+                    for e in range(e0, e0 + ne):
+                        mx_pass(c, e, halves[0], x, accs[e - e0][:])
+                for e in range(e0, e0 + ne):
+                    nc.scalar.activation(yt[:, e - e0], accs[e - e0][:], COPY, scale=gate_col[:, e : e + 1])
+            for n, h in enumerate(halves):
+                tr = psum.tile([P, ne * C], F32, name="tr", tag="tr", bufs=3)
+                for j in range(ne):
+                    nc.tensor.transpose(tr[:, j * C : (j + 1) * C], yt[:, j, n * C : (n + 1) * C], ident[:])
+                nc.scalar.copy(dx[h][:, e0 * C : (e0 + ne) * C], tr[:])
+
+        def combine(h):
+            half = T // 2
+            part = {}
+            for r in range(TOP):
+                for u in range(2):
+                    picked = dx[h][:].indirect(pos_sb[r][:, u * half // 16 : (u + 1) * half // 16])
+                    part[r, u] = new(f"part{h}{r}{u}", [P, half], F32)
+                    if r == 0:
+                        nc.vector.tensor_copy(part[r, u][:], picked)
+                    else:
+                        nc.vector.tensor_tensor(part[r, u][:], picked, part[r - 1, u][:], ADD)
+                    if r == TOP - 1:
+                        nc.sync.dma_start(out[h * P : (h + 1) * P, u * half : (u + 1) * half], part[r, u][:])
+
+        gather_w(0, "qkv")
+        gather_w(1, "qk")
+        gather_s(0, "qkv")
+        for e in range(4):
+            cast(e)
+        quant(0)
+        quant(1)
+        gather_w(1, "v")
+        gather_s(1, "qkv")
+        for e in range(4, 8):
+            cast(e)
+        products(0, (0, 1))
+        quant(2)
+        quant(3)
+        gather_w(2, "qkv")
+        cast(8)
+        cast(9)
+        quant(4)
+        gather_s(2, "qk")
+        cast(10)
+        cast(11)
+        products(1, (0, 1))
+        quant(5)
+        gather_s(2, "v")
+        gather_w(3, "qkv")
+        gather_s(3, "qkv")
+        cast(12)
+        cast(13)
+        quant(6)
+        gather_w(4, "qkv")
+        cast(14)
+        cast(15)
+        quant(7)
+        gather_s(4, "qkv")
+        products(2, (0, 1))
+        products(3, (0,))
+        products(4, (0,))
+        quant_late()
+        combine(0)
+        products(3, (1,))
+        products(4, (1,))
+        combine(1)

@@ -19,10 +19,10 @@ COPY = mybir.ActivationFunctionType.Copy
 ADD = mybir.AluOpType.add
 
 P = 128
-WINDOW = 704
+WINDOW = 1408
+WIDE = 8
 LINE = 64
-CHUNKS = [(0, 4), (4, 4), (8, 4), (12, 2), (14, 2)]
-LATE = 12
+LATE = 6
 SCALE_SPAN = 8
 
 
@@ -47,21 +47,17 @@ def tile_moe_qkb_kernel(
 ):
     nc = tc.nc
 
-    def wsz(c):
-        return CHUNKS[c][1] * C * 4
-
-    def ssz(c):
-        return CHUNKS[c][1] * C
-
+    wide_w = WIDE * C * 4
+    wide_s = WIDE * C
     tenants = {
-        "bf1": [("gw1v", wsz(1)), ("gs1q", ssz(1)), ("gs1k", ssz(1)), ("gs1v", ssz(1))],
-        "bf3": [("gw2q", wsz(2)), ("gw2k", wsz(2)), ("gw2v", wsz(2))],
-        "bf4": [("gs2q", ssz(2)), ("gs2k", ssz(2))],
-        "bf5": [("gw3q", wsz(3)), ("gs2v", ssz(2)), ("gw3k", wsz(3)), ("gs3q", ssz(3)), ("gs3k", ssz(3)), ("gs3v", ssz(3)), ("gw3v", wsz(3))],
-        "raw13": [("gw4q", wsz(4)), ("gw4k", wsz(4)), ("gw4v", wsz(4))],
-        "raw15": [("gs4q", ssz(4)), ("gs4k", ssz(4)), ("gs4v", ssz(4)), ("y2", 4096)],
-        "raw7": [("y0", 4096)],
-        "raw11": [("y1", 4096)],
+        "bf1": [("gsk0", wide_s)],
+        "raw5": [("gsv0", 4 * C)],
+        "raw7": [("gwq8", wide_w), ("gsv4", 4 * C), ("gwk8", wide_w)],
+        "raw9": [("gwv8", wide_w), ("gsq8", wide_s), ("y4h0", 2048), ("y6h0", 1024)],
+        "raw11": [("gsk8", wide_s), ("gsv8", 4 * C)],
+        "raw13": [("gsv12", 2 * C)],
+        "raw15": [("gsv14", 2 * C), ("y8h0", 2048)],
+        "raw8": [("y0h0", 4096)],
         "swinv": [("late_codes", (E - LATE) * C * 4)],
     }
     hosts = [(f"raw{e}", 4096, tenants.get(f"raw{e}", [])) for e in range(E)]
@@ -92,8 +88,6 @@ def tile_moe_qkb_kernel(
         for x in "qkv":
             nc.vector.memset(swin[x][:].bitcast(I32), 0)
         nc.gpsimd.memset(gate_rows[:], 0.0)
-        for x in "qkv":
-            nc.vector.memset(wwin[x][:, T:], 0)
         for x in "qv":
             nc.vector.memset(wplane[x, 0][:].bitcast(I32), 0)
         for x in "qv":
@@ -133,29 +127,31 @@ def tile_moe_qkb_kernel(
 
         nc.sync.dma_start(offs_sb[:], offs)
         load_words("q")
+        load_wk(0)
         load_words("k")
         nc.sync.dma_start(gate_rows[:E, :], gate[0:1, :].rearrange("o (e u) -> (o e) u", e=E))
-        load_words("v")
-        load_wk(0)
-        load_scales("q")
         load_wk(1)
-        load_scales("k")
+        load_words("v")
+        load_scales("q")
         load_wk(2)
-        load_scales("v")
         load_wk(3)
+        load_scales("k")
+        load_wk(4)
+        load_scales("v")
+        load_wk(5)
         load_w4_scales("q", 0)
-        load_w4(0)
+        load_wk(6)
         load_w4_scales("v", 0)
-        for e in range(4, 8):
-            load_wk(e)
+        load_wk(7)
+        load_wk(8)
+        load_w4(0)
+        load_wk(9)
         load_w4(1)
-        for e in range(8, 12):
+        for e in range(10, 16):
             load_wk(e)
         load_w4_scales("q", 1)
         load_w4(2)
         load_w4_scales("v", 1)
-        for e in range(12, 16):
-            load_wk(e)
         load_w4(3)
         for r, pos in enumerate((pos1, pos2, pos3, pos4)):
             nc.sync.dma_start(pos_sb[r][:], pos)
@@ -211,22 +207,19 @@ def tile_moe_qkb_kernel(
                 nc.vector.quantize_mx(out=codes[e, 1].bitcast(FP8X4), scales=kscale[e, 1],
                                       in_=flat[:, (2 * j + 1) * 4 * C : (2 * j + 2) * 4 * C])
 
-        def chunk_offsets(c):
-            e0, ne = CHUNKS[c]
-            return offs_sb[:, e0 * C // 16 : (e0 + ne) * C // 16]
+        def gather_w(x, e0, ne):
+            got = new(f"gw{x}{e0}", [P, ne * C], U32)
+            nc.vector.tensor_copy(got[:], wwin[x][:].bitcast(U32).indirect(offs_sb[:, e0 * C // 16 : (e0 + ne) * C // 16]))
+            for j in range(ne):
+                gw[x, e0 + j] = got[:, j * C : (j + 1) * C]
 
-        def gather_w(c, xs):
-            for x in xs:
-                gw[c, x] = new(f"gw{c}{x}", [P, CHUNKS[c][1] * C], U32)
-                nc.vector.tensor_copy(gw[c, x][:], wwin[x][:].bitcast(U32).indirect(chunk_offsets(c)))
+        def gather_s(x, e0, ne):
+            got = new(f"gs{x}{e0}", [P, ne * C], U8)
+            nc.vector.tensor_copy(got[:], swin[x][:].indirect(offs_sb[:, e0 * C // 16 : (e0 + ne) * C // 16]))
+            for j in range(ne):
+                gs[x, e0 + j] = got[:, j * C : (j + 1) * C]
 
-        def gather_s(c, xs):
-            for x in xs:
-                gs[c, x] = new(f"gs{c}{x}", [P, CHUNKS[c][1] * C], U8)
-                nc.vector.tensor_copy(gs[c, x][:], swin[x][:].indirect(chunk_offsets(c)))
-
-        def mx_pass(c, e, h, x, acc):
-            slots = slice((e - CHUNKS[c][0]) * C, (e - CHUNKS[c][0] + 1) * C)
+        def mx_pass(e, h, x, acc):
             if x == "k":
                 rhs, rhs_scale = codes[e, h].bitcast(FP8X4), kscale[e, h]
             else:
@@ -234,26 +227,25 @@ def tile_moe_qkb_kernel(
                 rhs = w4[x, e // 4][:, b0 : b0 + 2 * C].bitcast(FP4X4)
                 s0 = (e % SCALE_SPAN) * K + h * C
                 rhs_scale = wplane[x, e // SCALE_SPAN][:, s0 : s0 + C]
-            nc.tensor.matmul_mx(out=acc, lhsT=gw[c, x][:, slots].bitcast(FP8X4), lhsT_scale=gs[c, x][:, slots],
+            nc.tensor.matmul_mx(out=acc, lhsT=gw[x, e].bitcast(FP8X4), lhsT_scale=gs[x, e],
                                 rhs=rhs, rhs_scale=rhs_scale, start=(x == "q"), stop=(x == "v"))
 
-        def products(c, halves):
-            e0, ne = CHUNKS[c]
+        def products(e0, ne, halves):
             width = len(halves) * C
-            name = f"y{c}" if len(halves) == 2 else f"y{c}h{halves[0]}"
+            name = f"y{e0}h{halves[0]}"
             yt = new(name, [P, ne, width], F32)
-            if len(halves) == 2:
+            if (e0 + ne, halves) != (E, (0,)):
                 for e in range(e0, e0 + ne):
                     acc = psum.tile([P, width], F32, name="acc", tag="acc", bufs=4)
-                    for h in halves:
+                    for n, h in enumerate(halves):
                         for x in "qkv":
-                            mx_pass(c, e, h, x, acc[:, h * C : (h + 1) * C])
+                            mx_pass(e, h, x, acc[:, n * C : (n + 1) * C])
                     nc.scalar.activation(yt[:, e - e0], acc[:], COPY, scale=gate_col[:, e : e + 1])
             else:
                 accs = [psum.tile([P, width], F32, name="acc", tag="acc", bufs=4) for e in range(ne)]
                 for x in "qkv":
                     for e in range(e0, e0 + ne):
-                        mx_pass(c, e, halves[0], x, accs[e - e0][:])
+                        mx_pass(e, halves[0], x, accs[e - e0][:])
                 for e in range(e0, e0 + ne):
                     nc.scalar.activation(yt[:, e - e0], accs[e - e0][:], COPY, scale=gate_col[:, e : e + 1])
             for n, h in enumerate(halves):
@@ -268,7 +260,7 @@ def tile_moe_qkb_kernel(
             for r in range(TOP):
                 for u in range(2):
                     picked = dx[h][:].indirect(pos_sb[r][:, u * half // 16 : (u + 1) * half // 16])
-                    part[r, u] = new(f"part{h}{r}{u}", [P, half], F32)
+                    part[r, u] = new(f"part{r}{u}" if r < TOP - 1 else f"done{h}{u}", [P, half], F32)
                     if r == 0:
                         nc.vector.tensor_copy(part[r, u][:], picked)
                     else:
@@ -276,45 +268,47 @@ def tile_moe_qkb_kernel(
                     if r == TOP - 1:
                         nc.sync.dma_start(out[h * P : (h + 1) * P, u * half : (u + 1) * half], part[r, u][:])
 
-        gather_w(0, "qkv")
-        gather_w(1, "qk")
-        gather_s(0, "qkv")
-        for e in range(4):
+        for x in "qkv":
+            gather_w(x, 0, WIDE)
+        gather_s("q", 0, WIDE)
+        for e in range(8):
             cast(e)
         quant(0)
         quant(1)
-        gather_w(1, "v")
-        gather_s(1, "qkv")
-        for e in range(4, 8):
-            cast(e)
-        products(0, (0, 1))
+        gather_s("k", 0, WIDE)
         quant(2)
+        gather_s("v", 0, 4)
         quant(3)
-        gather_w(2, "qkv")
+        gather_s("v", 4, 4)
+        gather_w("q", 8, WIDE)
+        gather_w("k", 8, WIDE)
         cast(8)
+        products(0, 4, (0, 1))
         cast(9)
         quant(4)
-        gather_s(2, "qk")
+        products(4, 2, (0, 1))
+        products(6, 2, (0,))
+        gather_w("v", 8, WIDE)
+        gather_s("q", 8, WIDE)
         cast(10)
         cast(11)
-        products(1, (0, 1))
         quant(5)
-        gather_s(2, "v")
-        gather_w(3, "qkv")
-        gather_s(3, "qkv")
+        gather_s("k", 8, WIDE)
+        gather_s("v", 8, 4)
         cast(12)
         cast(13)
         quant(6)
-        gather_w(4, "qkv")
+        gather_s("v", 12, 2)
         cast(14)
         cast(15)
         quant(7)
-        gather_s(4, "qkv")
-        products(2, (0, 1))
-        products(3, (0,))
-        products(4, (0,))
+        gather_s("v", 14, 2)
+        products(8, 4, (0,))
+        products(12, 2, (0,))
+        products(14, 2, (0,))
         quant_late()
+        products(6, 2, (1,))
+        products(8, 4, (1,))
+        products(12, 4, (1,))
         combine(0)
-        products(3, (1,))
-        products(4, (1,))
         combine(1)

@@ -51,16 +51,15 @@ def tile_moe_qkb_kernel(
     wide_s = WIDE * C
     tenants = {
         "bf1": [("gsk0", wide_s)],
-        "raw5": [("gsv0", 4 * C)],
-        "raw7": [("gwq8", wide_w), ("gsv4", 4 * C), ("gwk8", wide_w)],
-        "raw9": [("gwv8", wide_w), ("gsq8", wide_s), ("y4h0", 2048), ("y6h0", 1024)],
-        "raw11": [("gsk8", wide_s), ("gsv8", 4 * C)],
-        "raw13": [("gsv12", 2 * C)],
-        "raw15": [("gsv14", 2 * C), ("y8h0", 2048)],
-        "raw8": [("y0h0", 4096)],
+        "bf2": [("gsv0", 4 * C)],
+        "raw3": [("gwq8", wide_w), ("gsv4", 4 * C), ("gwk8", wide_w), ("y0h0", 4096)],
+        "raw4": [("gwv8", wide_w), ("gsq8", wide_s), ("y4h0", 2048), ("y6h0", 1024)],
+        "raw5": [("gsk8", 4 * C), ("gsv8", 4 * C), ("gsk12", 4 * C)],
+        "raw6": [("gsv12", 2 * C)],
+        "raw7": [("gsv14", 2 * C), ("y8h0", 2048)],
         "swinv": [("late_codes", (E - LATE) * C * 4)],
     }
-    hosts = [(f"raw{e}", 4096, tenants.get(f"raw{e}", [])) for e in range(E)]
+    hosts = [(f"raw{i}", 8192, tenants.get(f"raw{i}", [])) for i in range(E // 2)]
     hosts = hosts + [(f"bf{i}", 4096, tenants.get(f"bf{i}", [])) for i in range(E // 2)]
     hosts = hosts + [("swinv", WINDOW, tenants["swinv"])]
     place = lay_out(hosts)
@@ -81,16 +80,15 @@ def tile_moe_qkb_kernel(
 
         wwin = {x: new(f"wwin{x}", [P, WINDOW], I32) for x in "qkv"}
         swin = {x: new(f"swin{x}", [P, WINDOW], U8) for x in "qkv"}
-        wplane = {(x, s): new(f"wplane{x}{s}", [P, SCALE_SPAN * K], U8) for x in "qv" for s in range(E // SCALE_SPAN)}
+        wplane = {(x, s): new(f"wplane{x}{s}", [P, SCALE_SPAN * K], U8) for s in range(E // SCALE_SPAN) for x in "qv"}
         gate_rows = new("gate_rows", [P, C], F32)
         ident = new("ident", [P, P], F32)
 
         for x in "qkv":
-            nc.vector.memset(swin[x][:].bitcast(I32), 0)
+            nc.vector.memset(swin[x][:].bitcast(I32)[:, : T // 4], 0)
         nc.gpsimd.memset(gate_rows[:], 0.0)
         for x in "qv":
             nc.vector.memset(wplane[x, 0][:].bitcast(I32), 0)
-        for x in "qv":
             nc.gpsimd.memset(wplane[x, 1][:].bitcast(I32), 0)
         make_identity(nc, ident[:])
 
@@ -109,15 +107,14 @@ def tile_moe_qkb_kernel(
             for r in range(4):
                 nc.sync.dma_start(swin[x][:].bitcast(I32)[r:P:32, : T // 4], src[r])
 
-        def load_wk(e):
-            raw[e] = new(f"raw{e}", [P, 4, K], F32)
-            nc.sync.dma_start(raw[e][:], wk[e].rearrange("(p j) c -> p j c", j=4))
+        def load_wk(i):
+            raw[i] = new(f"raw{i}", [P, 2, 4 * K], F32)
+            nc.sync.dma_start(raw[i][:], wk[2 * i : 2 * i + 2].rearrange("e (p j) c -> p e (j c)", j=4))
 
-        def load_w4(g):
-            for x in "qv":
-                w4[x, g] = new(f"w4{x}{g}", [P, 4 * 2 * K], U8)
-                src = w4_in[x][4 * g : 4 * g + 4, 0].bitcast(I32).rearrange("e p b -> p e b")
-                nc.sync.dma_start(w4[x, g][:].bitcast(I32).rearrange("p (e b) -> p e b", e=4), src)
+        def load_w4(x, g):
+            w4[x, g] = new(f"w4{x}{g}", [P, 4 * 2 * K], U8)
+            src = w4_in[x][4 * g : 4 * g + 4, 0].bitcast(I32).rearrange("e p b -> p e b")
+            nc.sync.dma_start(w4[x, g][:].bitcast(I32).rearrange("p (e b) -> p e b", e=4), src)
 
         def load_w4_scales(x, s):
             src = w4s_in[x][SCALE_SPAN * s : SCALE_SPAN * (s + 1), 0].bitcast(I32).rearrange("e (q r) c -> r q e c", r=4)
@@ -125,34 +122,33 @@ def tile_moe_qkb_kernel(
             for r in range(4):
                 nc.sync.dma_start(dst[r:P:32], src[r])
 
-        nc.sync.dma_start(offs_sb[:], offs)
         load_words("q")
-        load_wk(0)
+        nc.sync.dma_start(offs_sb[:], offs)
         load_words("k")
-        nc.sync.dma_start(gate_rows[:E, :], gate[0:1, :].rearrange("o (e u) -> (o e) u", e=E))
-        load_wk(1)
+        load_wk(0)
         load_words("v")
         load_scales("q")
-        load_wk(2)
-        load_wk(3)
+        load_wk(1)
         load_scales("k")
-        load_wk(4)
+        nc.sync.dma_start(gate_rows[:E, :], gate[0:1, :].rearrange("o (e u) -> (o e) u", e=E))
+        load_wk(2)
         load_scales("v")
-        load_wk(5)
+        load_wk(3)
         load_w4_scales("q", 0)
-        load_wk(6)
+        load_w4("q", 0)
         load_w4_scales("v", 0)
-        load_wk(7)
-        load_wk(8)
-        load_w4(0)
-        load_wk(9)
-        load_w4(1)
-        for e in range(10, 16):
-            load_wk(e)
+        load_w4("v", 0)
+        load_wk(4)
+        load_w4("q", 1)
+        load_w4("v", 1)
+        for i in range(5, 8):
+            load_wk(i)
         load_w4_scales("q", 1)
-        load_w4(2)
+        load_w4("q", 2)
+        load_w4("v", 2)
         load_w4_scales("v", 1)
-        load_w4(3)
+        load_w4("q", 3)
+        load_w4("v", 3)
         for r, pos in enumerate((pos1, pos2, pos3, pos4)):
             nc.sync.dma_start(pos_sb[r][:], pos)
 
@@ -176,7 +172,7 @@ def tile_moe_qkb_kernel(
                 bf[i] = new(f"bf{i}", [P, 2, K, 4], BF16)
             nc.scalar.copy(
                 bf[i][:, j].rearrange("p (c i) t -> p c t i", i=4),
-                raw[e][:].rearrange("p t (c i) -> p c t i", i=4),
+                raw[i][:, j].rearrange("p (t c i) -> p c t i", t=4, i=4),
             )
 
         def quant(i):
@@ -234,15 +230,15 @@ def tile_moe_qkb_kernel(
             width = len(halves) * C
             name = f"y{e0}h{halves[0]}"
             yt = new(name, [P, ne, width], F32)
-            if (e0 + ne, halves) != (E, (0,)):
+            if e0 < 12 or halves != (0,):
                 for e in range(e0, e0 + ne):
-                    acc = psum.tile([P, width], F32, name="acc", tag="acc", bufs=4)
+                    acc = psum.tile([P, width], F32, name="acc", tag="acc", bufs=5)
                     for n, h in enumerate(halves):
                         for x in "qkv":
                             mx_pass(e, h, x, acc[:, n * C : (n + 1) * C])
                     nc.scalar.activation(yt[:, e - e0], acc[:], COPY, scale=gate_col[:, e : e + 1])
             else:
-                accs = [psum.tile([P, width], F32, name="acc", tag="acc", bufs=4) for e in range(ne)]
+                accs = [psum.tile([P, width], F32, name="acc", tag="acc", bufs=5) for e in range(ne)]
                 for x in "qkv":
                     for e in range(e0, e0 + ne):
                         mx_pass(e, halves[0], x, accs[e - e0][:])
@@ -282,8 +278,8 @@ def tile_moe_qkb_kernel(
         gather_s("v", 4, 4)
         gather_w("q", 8, WIDE)
         gather_w("k", 8, WIDE)
-        cast(8)
         products(0, 4, (0, 1))
+        cast(8)
         cast(9)
         quant(4)
         products(4, 2, (0, 1))
@@ -293,8 +289,9 @@ def tile_moe_qkb_kernel(
         cast(10)
         cast(11)
         quant(5)
-        gather_s("k", 8, WIDE)
+        gather_s("k", 8, 4)
         gather_s("v", 8, 4)
+        gather_s("k", 12, 4)
         cast(12)
         cast(13)
         quant(6)
@@ -309,6 +306,7 @@ def tile_moe_qkb_kernel(
         quant_late()
         products(6, 2, (1,))
         products(8, 4, (1,))
-        products(12, 4, (1,))
+        products(12, 2, (1,))
+        products(14, 2, (1,))
         combine(0)
         combine(1)

@@ -19,25 +19,31 @@ COPY = mybir.ActivationFunctionType.Copy
 ADD = mybir.AluOpType.add
 
 P = 128
+PACK = 4
+PER_COLUMN = 16
+ALIGN = 64
+PAIR = 2
+QUAD = 4
+OCT = 8
 WINDOW = 1408
-WIDE = 8
-LINE = 64
-LATE = 6
-SCALE_SPAN = 8
+LATE = 8
+ACC_BANKS = 5
+TURN_BANKS = 3
 
 
 def lay_out(hosts):
     place = {}
     top = 0
-    for name, size, tenants in hosts:
-        lead = tenants[0][1] - LINE if tenants else 0
+    for name, size, followers in hosts:
+        lead = followers[0][1] - ALIGN if followers else 0
         place[name] = top + lead
+        host_end = top + lead + size
         at = top
-        for tenant, tenant_size in tenants:
-            assert at < top + lead + size
-            place[tenant] = at
-            at = at + tenant_size
-        top = max(at, top + lead + size)
+        for follower, follower_size in followers:
+            assert at < host_end
+            place[follower] = at
+            at = at + follower_size
+        top = max(at, host_end)
     return place
 
 
@@ -47,266 +53,275 @@ def tile_moe_qkb_kernel(
 ):
     nc = tc.nc
 
-    wide_w = WIDE * C * 4
-    wide_s = WIDE * C
-    tenants = {
-        "bf1": [("gsk0", wide_s)],
-        "bf2": [("gsv0", 4 * C)],
-        "raw3": [("gwq8", wide_w), ("gsv4", 4 * C), ("gwk8", wide_w), ("y0h0", 4096)],
-        "raw4": [("gwv8", wide_w), ("gsq8", wide_s), ("y4h0", 2048), ("y6h0", 1024)],
-        "raw5": [("gsk8", 4 * C), ("gsv8", 4 * C), ("gsk12", 4 * C)],
-        "raw6": [("gsv12", 2 * C)],
-        "raw7": [("gsv14", 2 * C), ("y8h0", 2048)],
-        "swinv": [("late_codes", (E - LATE) * C * 4)],
+    def words(x, e0, count):
+        return (f"words_{x}{e0}", count * C * PACK)
+
+    def scales(x, e0, count):
+        return (f"scales_{x}{e0}", count * C)
+
+    def gated(e0, count, halves):
+        return (f"gated{e0}_0", count * halves * P * 4)
+
+    followers = {
+        "rounded1": [scales("k", 0, OCT)],
+        "rounded2": [scales("v", 0, QUAD)],
+        "rounded3": [words("q", 8, OCT), scales("v", 4, QUAD), words("k", 8, OCT)],
+        "raw4": [words("v", 8, OCT), scales("q", 8, OCT), gated(0, QUAD, 2), gated(4, QUAD, 2)],
+        "raw5": [scales("k", 8, QUAD), scales("v", 8, QUAD), scales("k", 12, QUAD)],
+        "raw6": [scales("v", 12, PAIR)],
+        "raw7": [scales("v", 14, PAIR), gated(8, QUAD, 1)],
+        "token_scales_v": [("late_codes", (E - LATE) * P * PACK)],
     }
-    hosts = [(f"raw{i}", 8192, tenants.get(f"raw{i}", [])) for i in range(E // 2)]
-    hosts = hosts + [(f"bf{i}", 4096, tenants.get(f"bf{i}", [])) for i in range(E // 2)]
-    hosts = hosts + [("swinv", WINDOW, tenants["swinv"])]
-    place = lay_out(hosts)
+    sizes = {f"raw{i}": PAIR * PACK * K * 4 for i in range(E // PAIR)}
+    sizes.update({f"rounded{i}": PAIR * PACK * K * 2 for i in range(E // PAIR)})
+    sizes["token_scales_v"] = WINDOW
+    place = lay_out([(name, size, followers.get(name, [])) for name, size in sizes.items()])
 
     with ExitStack() as ctx:
         lists = ctx.enter_context(tc.tile_pool(name="lists", bufs=1))
         keep = ctx.enter_context(tc.tile_pool(name="keep", bufs=1))
-        shared = ctx.enter_context(tc.tile_pool(name="shared", bufs=1))
+        reused = ctx.enter_context(tc.tile_pool(name="reused", bufs=1))
         psum = ctx.enter_context(tc.psum_pool(name="psum", bufs=1))
 
         def new(name, shape, dtype):
             if name in place:
-                return shared.tile(shape, dtype, name=name, offset=place[name], align_bytes=LINE)
-            return keep.tile(shape, dtype, name=name, align_bytes=LINE)
+                return reused.tile(shape, dtype, name=name, offset=place[name], align_bytes=ALIGN)
+            return keep.tile(shape, dtype, name=name, align_bytes=ALIGN)
 
-        offs_sb = lists.tile([P, SLOTS // 16], U16, name="offs_sb")
-        pos_sb = [lists.tile([P, T // 16], U16, name=f"pos_sb{r}") for r in range(TOP)]
+        offs_sb = lists.tile([P, SLOTS // PER_COLUMN], U16, name="offs_sb")
+        pos_sb = [lists.tile([P, T // PER_COLUMN], U16, name=f"pos_sb{r}") for r in range(TOP)]
 
-        wwin = {x: new(f"wwin{x}", [P, WINDOW], I32) for x in "qkv"}
-        swin = {x: new(f"swin{x}", [P, WINDOW], U8) for x in "qkv"}
-        wplane = {(x, s): new(f"wplane{x}{s}", [P, SCALE_SPAN * K], U8) for s in range(E // SCALE_SPAN) for x in "qv"}
+        token_words = {x: new(f"token_words_{x}", [P, WINDOW], I32) for x in "qkv"}
+        token_scales = {x: new(f"token_scales_{x}", [P, WINDOW], U8) for x in "qkv"}
+        plane4 = {(x, s): new(f"plane4_{x}{s}", [P, OCT * K], U8) for s in range(E // OCT) for x in "qv"}
         gate_rows = new("gate_rows", [P, C], F32)
         ident = new("ident", [P, P], F32)
 
         for x in "qkv":
-            nc.vector.memset(swin[x][:].bitcast(I32)[:, : T // 4], 0)
+            nc.vector.memset(token_scales[x][:].bitcast(I32)[:, : T // 4], 0)
         nc.gpsimd.memset(gate_rows[:], 0.0)
         for x in "qv":
-            nc.vector.memset(wplane[x, 0][:].bitcast(I32), 0)
-            nc.gpsimd.memset(wplane[x, 1][:].bitcast(I32), 0)
+            nc.vector.memset(plane4[x, 0][:].bitcast(I32), 0)
+            nc.gpsimd.memset(plane4[x, 1][:].bitcast(I32), 0)
         make_identity(nc, ident[:])
 
         words_in = {"q": dq_words, "k": dk_words, "v": dv_words}
         scales_in = {"q": dq_scales, "k": dk_scales, "v": dv_scales}
-        w4_in = {"q": wq_words, "v": wv_words}
-        w4s_in = {"q": wq_scales, "v": wv_scales}
+        words4_in = {"q": wq_words, "v": wv_words}
+        scales4_in = {"q": wq_scales, "v": wv_scales}
         raw = {}
-        w4 = {}
+        words4 = {}
 
-        def load_words(x):
-            nc.sync.dma_start(wwin[x][:, :T], words_in[x][0].rearrange("p t d -> p (t d)").bitcast(I32))
+        def load_token_words(x):
+            nc.sync.dma_start(token_words[x][:, :T], words_in[x][0].rearrange("p t d -> p (t d)").bitcast(I32))
 
-        def load_scales(x):
+        def load_token_scales(x):
             src = scales_in[x][0].bitcast(I32).rearrange("(q r) t -> r q t", r=4)
             for r in range(4):
-                nc.sync.dma_start(swin[x][:].bitcast(I32)[r:P:32, : T // 4], src[r])
+                nc.sync.dma_start(token_scales[x][:].bitcast(I32)[r:P:32, : T // 4], src[r])
 
         def load_wk(i):
-            raw[i] = new(f"raw{i}", [P, 2, 4 * K], F32)
-            nc.sync.dma_start(raw[i][:], wk[2 * i : 2 * i + 2].rearrange("e (p j) c -> p e (j c)", j=4))
+            raw[i] = new(f"raw{i}", [P, PAIR, PACK * K], F32)
+            nc.sync.dma_start(raw[i][:], wk[PAIR * i : PAIR * (i + 1)].rearrange("e (p t) c -> p e (t c)", t=PACK))
 
-        def load_w4(x, g):
-            w4[x, g] = new(f"w4{x}{g}", [P, 4 * 2 * K], U8)
-            src = w4_in[x][4 * g : 4 * g + 4, 0].bitcast(I32).rearrange("e p b -> p e b")
-            nc.sync.dma_start(w4[x, g][:].bitcast(I32).rearrange("p (e b) -> p e b", e=4), src)
+        def load_words4(x, g):
+            words4[x, g] = new(f"words4_{x}{g}", [P, QUAD * 2 * K], U8)
+            src = words4_in[x][QUAD * g : QUAD * (g + 1), 0].bitcast(I32).rearrange("e p b -> p e b")
+            nc.sync.dma_start(words4[x, g][:].bitcast(I32).rearrange("p (e b) -> p e b", e=QUAD), src)
 
-        def load_w4_scales(x, s):
-            src = w4s_in[x][SCALE_SPAN * s : SCALE_SPAN * (s + 1), 0].bitcast(I32).rearrange("e (q r) c -> r q e c", r=4)
-            dst = wplane[x, s][:].bitcast(I32).rearrange("p (e c) -> p e c", e=SCALE_SPAN)
+        def load_scales4(x, s):
+            src = scales4_in[x][OCT * s : OCT * (s + 1), 0].bitcast(I32).rearrange("e (q r) c -> r q e c", r=4)
+            dst = plane4[x, s][:].bitcast(I32).rearrange("p (e c) -> p e c", e=OCT)
             for r in range(4):
                 nc.sync.dma_start(dst[r:P:32], src[r])
 
-        load_words("q")
+        load_token_words("q")
         nc.sync.dma_start(offs_sb[:], offs)
-        load_words("k")
+        load_token_words("k")
         load_wk(0)
-        load_words("v")
-        load_scales("q")
+        load_token_words("v")
+        load_token_scales("q")
         load_wk(1)
-        load_scales("k")
+        load_token_scales("k")
         nc.sync.dma_start(gate_rows[:E, :], gate[0:1, :].rearrange("o (e u) -> (o e) u", e=E))
         load_wk(2)
-        load_scales("v")
+        load_token_scales("v")
         load_wk(3)
-        load_w4_scales("q", 0)
-        load_w4("q", 0)
-        load_w4_scales("v", 0)
-        load_w4("v", 0)
+        load_scales4("q", 0)
         load_wk(4)
-        load_w4("q", 1)
-        load_w4("v", 1)
-        for i in range(5, 8):
+        load_scales4("v", 0)
+        for g in range(2):
+            for x in "qv":
+                load_words4(x, g)
+        for i in range(5, E // PAIR):
             load_wk(i)
-        load_w4_scales("q", 1)
-        load_w4("q", 2)
-        load_w4("v", 2)
-        load_w4_scales("v", 1)
-        load_w4("q", 3)
-        load_w4("v", 3)
+        load_scales4("q", 1)
+        for x in "qv":
+            load_words4(x, 2)
+        load_scales4("v", 1)
+        for x in "qv":
+            load_words4(x, 3)
         for r, pos in enumerate((pos1, pos2, pos3, pos4)):
             nc.sync.dma_start(pos_sb[r][:], pos)
 
-        gate_ps = psum.tile([P, P], F32, name="gate_ps", tag="tr", bufs=3)
-        nc.tensor.transpose(gate_ps[:], gate_rows[:], ident[:])
-        gate_col = new("gate_col", [P, E], F32)
-        nc.scalar.copy(gate_col[:], gate_ps[:, :E])
+        gate_turned = psum.tile([P, P], F32, name="gate_turned", tag="turn", bufs=TURN_BANKS)
+        nc.tensor.transpose(gate_turned[:], gate_rows[:], ident[:])
+        gate_cols = new("gate_cols", [P, E], F32)
+        nc.scalar.copy(gate_cols[:], gate_turned[:, :E])
 
-        bf = {}
-        codes = {}
-        kscale = {}
-        gw = {}
-        gs = {}
-        y = {}
+        rounded = {}
+        k_codes = {}
+        k_plane = {}
+        slot_words = {}
+        slot_scales = {}
         dx = [new(f"dx{h}", [P, SLOTS], F32) for h in range(2)]
-        late = {}
 
-        def cast(e):
-            i, j = divmod(e, 2)
-            if j == 0:
-                bf[i] = new(f"bf{i}", [P, 2, K, 4], BF16)
-            nc.scalar.copy(
-                bf[i][:, j].rearrange("p (c i) t -> p c t i", i=4),
-                raw[i][:, j].rearrange("p (t c i) -> p c t i", t=4, i=4),
+        def round_pair(i):
+            rounded[i] = new(f"rounded{i}", [P, PAIR, K, PACK], BF16)
+            for j in range(PAIR):
+                nc.scalar.copy(
+                    rounded[i][:, j].rearrange("p (c i) t -> p c t i", i=4),
+                    raw[i][:, j].rearrange("p (t c i) -> p c t i", t=PACK, i=4),
+                )
+
+        def quantise_both_halves(i):
+            codes = new(f"k_codes{i}", [P, PAIR * K], U32)
+            plane = new(f"k_plane{i}", [P, PAIR * K], U8)
+            nc.vector.quantize_mx(
+                out=codes[:].bitcast(FP8X4), scales=plane[:], in_=rounded[i][:].rearrange("p j c t -> p (j c t)")
+            )
+            for j in range(PAIR):
+                for h in range(2):
+                    cols = slice(j * K + h * P, j * K + (h + 1) * P)
+                    k_codes[PAIR * i + j, h] = codes[:, cols]
+                    k_plane[PAIR * i + j, h] = plane[:, cols]
+
+        def quantise_half(name, experts, h):
+            codes = new(f"{name}_codes", [P, len(experts) * P], U32)
+            plane = new(f"{name}_plane", [P, len(experts) * P], U8)
+            for n, e in enumerate(experts):
+                k_codes[e, h] = codes[:, n * P : (n + 1) * P]
+                k_plane[e, h] = plane[:, n * P : (n + 1) * P]
+                source = rounded[e // PAIR][:, e % PAIR, h * P : (h + 1) * P].rearrange("p c t -> p (c t)")
+                nc.vector.quantize_mx(out=k_codes[e, h].bitcast(FP8X4), scales=k_plane[e, h], in_=source)
+
+        def quantise_first_half(i):
+            quantise_half(f"first{i}", range(PAIR * i, PAIR * (i + 1)), 0)
+
+        def slots_of(e0, count):
+            return offs_sb[:, e0 * C // PER_COLUMN : (e0 + count) * C // PER_COLUMN]
+
+        def gather_words(x, e0, count):
+            got = new(words(x, e0, count)[0], [P, count * C], U32)
+            nc.vector.tensor_copy(got[:], token_words[x][:].bitcast(U32).indirect(slots_of(e0, count)))
+            for j in range(count):
+                slot_words[x, e0 + j] = got[:, j * C : (j + 1) * C]
+
+        def gather_scales(x, e0, count):
+            got = new(scales(x, e0, count)[0], [P, count * C], U8)
+            nc.vector.tensor_copy(got[:], token_scales[x][:].indirect(slots_of(e0, count)))
+            for j in range(count):
+                slot_scales[x, e0 + j] = got[:, j * C : (j + 1) * C]
+
+        def mx_pass(x, e, h, acc):
+            if x == "k":
+                moving, moving_plane = k_codes[e, h].bitcast(FP8X4), k_plane[e, h]
+            else:
+                byte0 = 2 * ((e % QUAD) * K + h * P)
+                moving = words4[x, e // QUAD][:, byte0 : byte0 + 2 * P].bitcast(FP4X4)
+                col0 = (e % OCT) * K + h * P
+                moving_plane = plane4[x, e // OCT][:, col0 : col0 + P]
+            nc.tensor.matmul_mx(
+                out=acc, lhsT=slot_words[x, e].bitcast(FP8X4), lhsT_scale=slot_scales[x, e],
+                rhs=moving, rhs_scale=moving_plane, start=(x == "q"), stop=(x == "v"),
             )
 
-        def quant(i):
-            ct = new(f"codes{i}", [P, 2 * K], U32)
-            st = new(f"kscale{i}", [P, 2 * K], U8)
-            flat = bf[i][:].rearrange("p j c t -> p (j c t)")
-            if 2 * i < LATE:
-                nc.vector.quantize_mx(out=ct[:].bitcast(FP8X4), scales=st[:], in_=flat)
-            for j in range(2):
-                for h in range(2):
-                    if 2 * i < LATE or h == 0:
-                        cols = slice((2 * j + h) * C, (2 * j + h + 1) * C)
-                        codes[2 * i + j, h] = ct[:, cols]
-                        kscale[2 * i + j, h] = st[:, cols]
-                if 2 * i >= LATE:
-                    nc.vector.quantize_mx(out=codes[2 * i + j, 0].bitcast(FP8X4), scales=kscale[2 * i + j, 0],
-                                          in_=flat[:, 2 * j * 4 * C : (2 * j + 1) * 4 * C])
+        def new_acc(width):
+            return psum.tile([P, width], F32, name="acc", tag="acc", bufs=ACC_BANKS)
 
-        def quant_late():
-            late["codes"] = new("late_codes", [P, (E - LATE) * C], U32)
-            late["scales"] = new("late_scales", [P, (E - LATE) * C], U8)
-            for e in range(LATE, E):
-                i, j = divmod(e, 2)
-                cols = slice((e - LATE) * C, (e - LATE + 1) * C)
-                codes[e, 1] = late["codes"][:, cols]
-                kscale[e, 1] = late["scales"][:, cols]
-                flat = bf[i][:].rearrange("p j c t -> p (j c t)")
-                nc.vector.quantize_mx(out=codes[e, 1].bitcast(FP8X4), scales=kscale[e, 1],
-                                      in_=flat[:, (2 * j + 1) * 4 * C : (2 * j + 2) * 4 * C])
+        def apply_gate(result, acc, e):
+            nc.scalar.activation(result, acc[:], COPY, scale=gate_cols[:, e : e + 1])
 
-        def gather_w(x, e0, ne):
-            got = new(f"gw{x}{e0}", [P, ne * C], U32)
-            nc.vector.tensor_copy(got[:], wwin[x][:].bitcast(U32).indirect(offs_sb[:, e0 * C // 16 : (e0 + ne) * C // 16]))
-            for j in range(ne):
-                gw[x, e0 + j] = got[:, j * C : (j + 1) * C]
-
-        def gather_s(x, e0, ne):
-            got = new(f"gs{x}{e0}", [P, ne * C], U8)
-            nc.vector.tensor_copy(got[:], swin[x][:].indirect(offs_sb[:, e0 * C // 16 : (e0 + ne) * C // 16]))
-            for j in range(ne):
-                gs[x, e0 + j] = got[:, j * C : (j + 1) * C]
-
-        def mx_pass(e, h, x, acc):
-            if x == "k":
-                rhs, rhs_scale = codes[e, h].bitcast(FP8X4), kscale[e, h]
-            else:
-                b0 = (e % 4) * 2 * K + h * 2 * C
-                rhs = w4[x, e // 4][:, b0 : b0 + 2 * C].bitcast(FP4X4)
-                s0 = (e % SCALE_SPAN) * K + h * C
-                rhs_scale = wplane[x, e // SCALE_SPAN][:, s0 : s0 + C]
-            nc.tensor.matmul_mx(out=acc, lhsT=gw[x, e].bitcast(FP8X4), lhsT_scale=gs[x, e],
-                                rhs=rhs, rhs_scale=rhs_scale, start=(x == "q"), stop=(x == "v"))
-
-        def products(e0, ne, halves):
-            width = len(halves) * C
-            name = f"y{e0}h{halves[0]}"
-            yt = new(name, [P, ne, width], F32)
-            if e0 < 12 or halves != (0,):
-                for e in range(e0, e0 + ne):
-                    acc = psum.tile([P, width], F32, name="acc", tag="acc", bufs=5)
-                    for n, h in enumerate(halves):
-                        for x in "qkv":
-                            mx_pass(e, h, x, acc[:, n * C : (n + 1) * C])
-                    nc.scalar.activation(yt[:, e - e0], acc[:], COPY, scale=gate_col[:, e : e + 1])
-            else:
-                accs = [psum.tile([P, width], F32, name="acc", tag="acc", bufs=5) for e in range(ne)]
-                for x in "qkv":
-                    for e in range(e0, e0 + ne):
-                        mx_pass(e, halves[0], x, accs[e - e0][:])
-                for e in range(e0, e0 + ne):
-                    nc.scalar.activation(yt[:, e - e0], accs[e - e0][:], COPY, scale=gate_col[:, e : e + 1])
+        def turn(result, e0, count, halves):
             for n, h in enumerate(halves):
-                tr = psum.tile([P, ne * C], F32, name="tr", tag="tr", bufs=3)
-                for j in range(ne):
-                    nc.tensor.transpose(tr[:, j * C : (j + 1) * C], yt[:, j, n * C : (n + 1) * C], ident[:])
-                nc.scalar.copy(dx[h][:, e0 * C : (e0 + ne) * C], tr[:])
+                turned = psum.tile([P, count * C], F32, name="turned", tag="turn", bufs=TURN_BANKS)
+                for j in range(count):
+                    nc.tensor.transpose(turned[:, j * C : (j + 1) * C], result[:, j, n * P : (n + 1) * P], ident[:])
+                nc.scalar.copy(dx[h][:, e0 * C : (e0 + count) * C], turned[:])
+
+        def products(e0, count, halves):
+            result = new(f"gated{e0}_{halves[0]}", [P, count, len(halves) * P], F32)
+            for j in range(count):
+                acc = new_acc(len(halves) * P)
+                for n, h in enumerate(halves):
+                    for x in "qkv":
+                        mx_pass(x, e0 + j, h, acc[:, n * P : (n + 1) * P])
+                apply_gate(result[:, j], acc, e0 + j)
+            turn(result, e0, count, halves)
+
+        def first_half_products_by_pass(e0):
+            result = new(f"gated{e0}_0", [P, PAIR, P], F32)
+            accs = [new_acc(P) for j in range(PAIR)]
+            for x in "qkv":
+                for j in range(PAIR):
+                    mx_pass(x, e0 + j, 0, accs[j][:])
+            for j in range(PAIR):
+                apply_gate(result[:, j], accs[j], e0 + j)
+            turn(result, e0, PAIR, (0,))
 
         def combine(h):
-            half = T // 2
-            part = {}
+            run = T // 2
+            total = {}
             for r in range(TOP):
                 for u in range(2):
-                    picked = dx[h][:].indirect(pos_sb[r][:, u * half // 16 : (u + 1) * half // 16])
-                    part[r, u] = new(f"part{r}{u}" if r < TOP - 1 else f"done{h}{u}", [P, half], F32)
+                    picked = dx[h][:].indirect(pos_sb[r][:, u * run // PER_COLUMN : (u + 1) * run // PER_COLUMN])
+                    last = r == TOP - 1
+                    total[r, u] = new(f"total{h}{u}" if last else f"partial{r}{u}", [P, run], F32)
                     if r == 0:
-                        nc.vector.tensor_copy(part[r, u][:], picked)
+                        nc.vector.tensor_copy(total[r, u][:], picked)
                     else:
-                        nc.vector.tensor_tensor(part[r, u][:], picked, part[r - 1, u][:], ADD)
-                    if r == TOP - 1:
-                        nc.sync.dma_start(out[h * P : (h + 1) * P, u * half : (u + 1) * half], part[r, u][:])
+                        nc.vector.tensor_tensor(total[r, u][:], picked, total[r - 1, u][:], ADD)
+                    if last:
+                        nc.sync.dma_start(out[h * P : (h + 1) * P, u * run : (u + 1) * run], total[r, u][:])
 
         for x in "qkv":
-            gather_w(x, 0, WIDE)
-        gather_s("q", 0, WIDE)
-        for e in range(8):
-            cast(e)
-        quant(0)
-        quant(1)
-        gather_s("k", 0, WIDE)
-        quant(2)
-        gather_s("v", 0, 4)
-        quant(3)
-        gather_s("v", 4, 4)
-        gather_w("q", 8, WIDE)
-        gather_w("k", 8, WIDE)
-        products(0, 4, (0, 1))
-        cast(8)
-        cast(9)
-        quant(4)
-        products(4, 2, (0, 1))
-        products(6, 2, (0,))
-        gather_w("v", 8, WIDE)
-        gather_s("q", 8, WIDE)
-        cast(10)
-        cast(11)
-        quant(5)
-        gather_s("k", 8, 4)
-        gather_s("v", 8, 4)
-        gather_s("k", 12, 4)
-        cast(12)
-        cast(13)
-        quant(6)
-        gather_s("v", 12, 2)
-        cast(14)
-        cast(15)
-        quant(7)
-        gather_s("v", 14, 2)
-        products(8, 4, (0,))
-        products(12, 2, (0,))
-        products(14, 2, (0,))
-        quant_late()
-        products(6, 2, (1,))
-        products(8, 4, (1,))
-        products(12, 2, (1,))
-        products(14, 2, (1,))
+            gather_words(x, 0, OCT)
+        gather_scales("q", 0, OCT)
+        for i in range(LATE // PAIR):
+            round_pair(i)
+        quantise_both_halves(0)
+        quantise_both_halves(1)
+        gather_scales("k", 0, OCT)
+        quantise_both_halves(2)
+        gather_scales("v", 0, QUAD)
+        quantise_both_halves(3)
+        gather_scales("v", 4, QUAD)
+        gather_words("q", 8, OCT)
+        gather_words("k", 8, OCT)
+        round_pair(4)
+        quantise_first_half(4)
+        products(0, QUAD, (0, 1))
+        products(4, QUAD, (0, 1))
+        gather_words("v", 8, OCT)
+        gather_scales("q", 8, OCT)
+        round_pair(5)
+        quantise_first_half(5)
+        gather_scales("k", 8, QUAD)
+        gather_scales("v", 8, QUAD)
+        gather_scales("k", 12, QUAD)
+        round_pair(6)
+        quantise_first_half(6)
+        gather_scales("v", 12, PAIR)
+        round_pair(7)
+        quantise_first_half(7)
+        gather_scales("v", 14, PAIR)
+        products(8, QUAD, (0,))
+        first_half_products_by_pass(12)
+        first_half_products_by_pass(14)
+
+        quantise_half("late", range(LATE, E), 1)
+        products(8, QUAD, (1,))
+        products(12, PAIR, (1,))
+        products(14, PAIR, (1,))
         combine(0)
         combine(1)

from contextlib import ExitStack

import concourse.mybir as mybir
from concourse.masks import make_identity

K, T, E, C, N, TOP = 256, 512, 16, 128, 512, 4
SLOTS = E * C
FLOPS = 2 * 3 * SLOTS * N * K

F32 = mybir.dt.float32
BF16 = mybir.dt.bfloat16
I32 = mybir.dt.int32
U32 = mybir.dt.uint32
U16 = mybir.dt.uint16
U8 = mybir.dt.uint8
FP8X4 = mybir.dt.float8_e4m3fn_x4
FP4X4 = mybir.dt.float4_e2m1fn_x4
COPY = mybir.ActivationFunctionType.Copy
ADD = mybir.AluOpType.add

P = 128
PACK = 4
PER_COLUMN = 16
ALIGN = 64
PAIR = 2
QUAD = 4
OCT = 8
WINDOW = 1408
LATE = 8
ACC_BANKS = 5
TURN_BANKS = 3


def lay_out(hosts):
    place = {}
    top = 0
    for name, size, followers in hosts:
        lead = followers[0][1] - ALIGN if followers else 0
        place[name] = top + lead
        host_end = top + lead + size
        at = top
        for follower, follower_size in followers:
            assert at < host_end
            place[follower] = at
            at = at + follower_size
        top = max(at, host_end)
    return place


def tile_moe_qkb_kernel(
    tc, dq_words, dq_scales, dk_words, dk_scales, dv_words, dv_scales, wq_words, wq_scales, wk, wv_words, wv_scales,
    gate, offs, pos1, pos2, pos3, pos4, out,
):
    nc = tc.nc

    def words(x, e0, count):
        return (f"words_{x}{e0}", count * C * PACK)

    def scales(x, e0, count):
        return (f"scales_{x}{e0}", count * C)

    def gated(e0, count, halves):
        return (f"gated{e0}_0", count * halves * P * 4)

    followers = {
        "rounded1": [scales("k", 0, OCT)],
        "rounded2": [scales("v", 0, QUAD)],
        "rounded3": [words("q", 8, OCT), scales("v", 4, QUAD), words("k", 8, OCT)],
        "raw4": [words("v", 8, OCT), scales("q", 8, OCT), gated(0, QUAD, 2), gated(4, QUAD, 2)],
        "raw5": [scales("k", 8, QUAD), scales("v", 8, QUAD), scales("k", 12, QUAD)],
        "raw6": [scales("v", 12, PAIR)],
        "raw7": [scales("v", 14, PAIR), gated(8, QUAD, 1)],
        "token_scales_v": [("late_codes", (E - LATE) * P * PACK)],
    }
    sizes = {f"raw{i}": PAIR * PACK * K * 4 for i in range(E // PAIR)}
    sizes.update({f"rounded{i}": PAIR * PACK * K * 2 for i in range(E // PAIR)})
    sizes["token_scales_v"] = WINDOW
    place = lay_out([(name, size, followers.get(name, [])) for name, size in sizes.items()])

    with ExitStack() as ctx:
        lists = ctx.enter_context(tc.tile_pool(name="lists", bufs=1))
        keep = ctx.enter_context(tc.tile_pool(name="keep", bufs=1))
        reused = ctx.enter_context(tc.tile_pool(name="reused", bufs=1))
        psum = ctx.enter_context(tc.psum_pool(name="psum", bufs=1))

        def new(name, shape, dtype):
            if name in place:
                return reused.tile(shape, dtype, name=name, offset=place[name], align_bytes=ALIGN)
            return keep.tile(shape, dtype, name=name, align_bytes=ALIGN)

        offs_sb = lists.tile([P, SLOTS // PER_COLUMN], U16, name="offs_sb")
        pos_sb = [lists.tile([P, T // PER_COLUMN], U16, name=f"pos_sb{r}") for r in range(TOP)]

        token_words = {x: new(f"token_words_{x}", [P, WINDOW], I32) for x in "qkv"}
        token_scales = {x: new(f"token_scales_{x}", [P, WINDOW], U8) for x in "qkv"}
        plane4 = {(x, s): new(f"plane4_{x}{s}", [P, OCT * K], U8) for s in range(E // OCT) for x in "qv"}
        gate_rows = new("gate_rows", [P, C], F32)
        ident = new("ident", [P, P], F32)

        for x in "qkv":
            nc.vector.memset(token_scales[x][:].bitcast(I32)[:, : T // 4], 0)
        nc.gpsimd.memset(gate_rows[:], 0.0)
        for x in "qv":
            nc.vector.memset(plane4[x, 0][:].bitcast(I32), 0)
            nc.gpsimd.memset(plane4[x, 1][:].bitcast(I32), 0)
        make_identity(nc, ident[:])

        words_in = {"q": dq_words, "k": dk_words, "v": dv_words}
        scales_in = {"q": dq_scales, "k": dk_scales, "v": dv_scales}
        words4_in = {"q": wq_words, "v": wv_words}
        scales4_in = {"q": wq_scales, "v": wv_scales}
        raw = {}
        words4 = {}

        def load_token_words(x):
            nc.sync.dma_start(token_words[x][:, :T], words_in[x][0].rearrange("p t d -> p (t d)").bitcast(I32))

        def load_token_scales(x):
            src = scales_in[x][0].bitcast(I32).rearrange("(q r) t -> r q t", r=4)
            for r in range(4):
                nc.sync.dma_start(token_scales[x][:].bitcast(I32)[r:P:32, : T // 4], src[r])

        def load_wk(i):
            raw[i] = new(f"raw{i}", [P, PAIR, PACK * K], F32)
            nc.sync.dma_start(raw[i][:], wk[PAIR * i : PAIR * (i + 1)].rearrange("e (p t) c -> p e (t c)", t=PACK))

        def load_words4(x, g):
            words4[x, g] = new(f"words4_{x}{g}", [P, QUAD * 2 * K], U8)
            src = words4_in[x][QUAD * g : QUAD * (g + 1), 0].bitcast(I32).rearrange("e p b -> p e b")
            nc.sync.dma_start(words4[x, g][:].bitcast(I32).rearrange("p (e b) -> p e b", e=QUAD), src)

        def load_scales4(x, s):
            src = scales4_in[x][OCT * s : OCT * (s + 1), 0].bitcast(I32).rearrange("e (q r) c -> r q e c", r=4)
            dst = plane4[x, s][:].bitcast(I32).rearrange("p (e c) -> p e c", e=OCT)
            for r in range(4):
                nc.sync.dma_start(dst[r:P:32], src[r])

        load_token_words("q")
        nc.sync.dma_start(offs_sb[:], offs)
        load_token_words("k")
        load_wk(0)
        load_token_words("v")
        load_token_scales("q")
        load_wk(1)
        load_token_scales("k")
        nc.sync.dma_start(gate_rows[:E, :], gate[0:1, :].rearrange("o (e u) -> (o e) u", e=E))
        load_wk(2)
        load_token_scales("v")
        load_wk(3)
        load_scales4("q", 0)
        load_wk(4)
        load_scales4("v", 0)
        for g in range(2):
            for x in "qv":
                load_words4(x, g)
        for i in range(5, E // PAIR):
            load_wk(i)
        load_scales4("q", 1)
        for x in "qv":
            load_words4(x, 2)
        load_scales4("v", 1)
        for x in "qv":
            load_words4(x, 3)
        for r, pos in enumerate((pos1, pos2, pos3, pos4)):
            nc.sync.dma_start(pos_sb[r][:], pos)

        gate_turned = psum.tile([P, P], F32, name="gate_turned", tag="turn", bufs=TURN_BANKS)
        nc.tensor.transpose(gate_turned[:], gate_rows[:], ident[:])
        gate_cols = new("gate_cols", [P, E], F32)
        nc.scalar.copy(gate_cols[:], gate_turned[:, :E])

        rounded = {}
        k_codes = {}
        k_plane = {}
        slot_words = {}
        slot_scales = {}
        dx = [new(f"dx{h}", [P, SLOTS], F32) for h in range(2)]

        def round_pair(i):
            rounded[i] = new(f"rounded{i}", [P, PAIR, K, PACK], BF16)
            for j in range(PAIR):
                nc.scalar.copy(
                    rounded[i][:, j].rearrange("p (c i) t -> p c t i", i=4),
                    raw[i][:, j].rearrange("p (t c i) -> p c t i", t=PACK, i=4),
                )

        def quantise_both_halves(i):
            codes = new(f"k_codes{i}", [P, PAIR * K], U32)
            plane = new(f"k_plane{i}", [P, PAIR * K], U8)
            nc.vector.quantize_mx(
                out=codes[:].bitcast(FP8X4), scales=plane[:], in_=rounded[i][:].rearrange("p j c t -> p (j c t)")
            )
            for j in range(PAIR):
                for h in range(2):
                    cols = slice(j * K + h * P, j * K + (h + 1) * P)
                    k_codes[PAIR * i + j, h] = codes[:, cols]
                    k_plane[PAIR * i + j, h] = plane[:, cols]

        def quantise_half(name, experts, h):
            codes = new(f"{name}_codes", [P, len(experts) * P], U32)
            plane = new(f"{name}_plane", [P, len(experts) * P], U8)
            for n, e in enumerate(experts):
                k_codes[e, h] = codes[:, n * P : (n + 1) * P]
                k_plane[e, h] = plane[:, n * P : (n + 1) * P]
                source = rounded[e // PAIR][:, e % PAIR, h * P : (h + 1) * P].rearrange("p c t -> p (c t)")
                nc.vector.quantize_mx(out=k_codes[e, h].bitcast(FP8X4), scales=k_plane[e, h], in_=source)

        def quantise_first_half(i):
            quantise_half(f"first{i}", range(PAIR * i, PAIR * (i + 1)), 0)

        def slots_of(e0, count):
            return offs_sb[:, e0 * C // PER_COLUMN : (e0 + count) * C // PER_COLUMN]

        def gather_words(x, e0, count):
            got = new(words(x, e0, count)[0], [P, count * C], U32)
            nc.vector.tensor_copy(got[:], token_words[x][:].bitcast(U32).indirect(slots_of(e0, count)))
            for j in range(count):
                slot_words[x, e0 + j] = got[:, j * C : (j + 1) * C]

        def gather_scales(x, e0, count):
            got = new(scales(x, e0, count)[0], [P, count * C], U8)
            nc.vector.tensor_copy(got[:], token_scales[x][:].indirect(slots_of(e0, count)))
            for j in range(count):
                slot_scales[x, e0 + j] = got[:, j * C : (j + 1) * C]

        def mx_pass(x, e, h, acc):
            if x == "k":
                moving, moving_plane = k_codes[e, h].bitcast(FP8X4), k_plane[e, h]
            else:
                byte0 = 2 * ((e % QUAD) * K + h * P)
                moving = words4[x, e // QUAD][:, byte0 : byte0 + 2 * P].bitcast(FP4X4)
                col0 = (e % OCT) * K + h * P
                moving_plane = plane4[x, e // OCT][:, col0 : col0 + P]
            nc.tensor.matmul_mx(
                out=acc, lhsT=slot_words[x, e].bitcast(FP8X4), lhsT_scale=slot_scales[x, e],
                rhs=moving, rhs_scale=moving_plane, start=(x == "q"), stop=(x == "v"),
            )

        def new_acc(width):
            return psum.tile([P, width], F32, name="acc", tag="acc", bufs=ACC_BANKS)

        def apply_gate(result, acc, e):
            nc.scalar.activation(result, acc[:], COPY, scale=gate_cols[:, e : e + 1])

        def turn(result, e0, count, halves):
            for n, h in enumerate(halves):
                turned = psum.tile([P, count * C], F32, name="turned", tag="turn", bufs=TURN_BANKS)
                for j in range(count):
                    nc.tensor.transpose(turned[:, j * C : (j + 1) * C], result[:, j, n * P : (n + 1) * P], ident[:])
                nc.scalar.copy(dx[h][:, e0 * C : (e0 + count) * C], turned[:])

        def products(e0, count, halves):
            result = new(f"gated{e0}_{halves[0]}", [P, count, len(halves) * P], F32)
            for j in range(count):
                acc = new_acc(len(halves) * P)
                for n, h in enumerate(halves):
                    for x in "qkv":
                        mx_pass(x, e0 + j, h, acc[:, n * P : (n + 1) * P])
                apply_gate(result[:, j], acc, e0 + j)
            turn(result, e0, count, halves)

        def first_half_products_by_pass(e0):
            result = new(f"gated{e0}_0", [P, PAIR, P], F32)
            accs = [new_acc(P) for j in range(PAIR)]
            for x in "qkv":
                for j in range(PAIR):
                    mx_pass(x, e0 + j, 0, accs[j][:])
            for j in range(PAIR):
                apply_gate(result[:, j], accs[j], e0 + j)
            turn(result, e0, PAIR, (0,))

        def combine(h):
            run = T // 2
            total = {}
            for r in range(TOP):
                for u in range(2):
                    picked = dx[h][:].indirect(pos_sb[r][:, u * run // PER_COLUMN : (u + 1) * run // PER_COLUMN])
                    last = r == TOP - 1
                    total[r, u] = new(f"total{h}{u}" if last else f"partial{r}{u}", [P, run], F32)
                    if r == 0:
                        nc.vector.tensor_copy(total[r, u][:], picked)
                    else:
                        nc.vector.tensor_tensor(total[r, u][:], picked, total[r - 1, u][:], ADD)
                    if last:
                        nc.sync.dma_start(out[h * P : (h + 1) * P, u * run : (u + 1) * run], total[r, u][:])

        for x in "qkv":
            gather_words(x, 0, OCT)
        gather_scales("q", 0, OCT)
        for i in range(LATE // PAIR):
            round_pair(i)
        quantise_both_halves(0)
        quantise_both_halves(1)
        gather_scales("k", 0, OCT)
        quantise_both_halves(2)
        gather_scales("v", 0, QUAD)
        quantise_both_halves(3)
        gather_scales("v", 4, QUAD)
        gather_words("q", 8, OCT)
        gather_words("k", 8, OCT)
        round_pair(4)
        quantise_first_half(4)
        products(0, QUAD, (0, 1))
        products(4, QUAD, (0, 1))
        gather_words("v", 8, OCT)
        gather_scales("q", 8, OCT)
        round_pair(5)
        quantise_first_half(5)
        gather_scales("k", 8, QUAD)
        gather_scales("v", 8, QUAD)
        gather_scales("k", 12, QUAD)
        round_pair(6)
        quantise_first_half(6)
        gather_scales("v", 12, PAIR)
        round_pair(7)
        quantise_first_half(7)
        gather_scales("v", 14, PAIR)
        products(8, QUAD, (0,))
        first_half_products_by_pass(12)
        first_half_products_by_pass(14)

        quantise_half("late", range(LATE, E), 1)
        products(8, QUAD, (1,))
        products(12, PAIR, (1,))
        products(14, PAIR, (1,))
        combine(0)
        combine(1)
